import numpy as np
import ml_dtypes


def mxq(x, axis, fmt="e4m3"):
    dtype, down = {"e4m3": (ml_dtypes.float8_e4m3fn, 7), "e5m2": (ml_dtypes.float8_e5m2, 14)}[fmt]
    v = np.moveaxis(np.asarray(x, np.float32).astype(ml_dtypes.bfloat16).astype(np.float64), axis, -1)
    blocks = v.reshape(v.shape[:-1] + (-1, 32))
    amax = np.abs(blocks).max(-1, keepdims=True)
    byte = np.maximum(np.where(amax > 0, np.frexp(amax)[1] - 1 + 127, 0) - down, 1)
    scale = np.exp2(byte - 127.0)
    codes = (blocks / scale).astype(np.float32).astype(dtype).astype(np.float64)
    return np.moveaxis((codes * scale).reshape(v.shape), -1, axis)


WIDE = False


def mx_kscale(k):
    if not WIDE:
        return np.ones(k)
    levels = np.array([30, -30])
    if k % 512:
        return np.exp2(np.random.permutation(np.resize(levels, k // 32))).repeat(32)
    a = np.empty((k // 512, 16))
    for p in range(k // 512):
        a[p, :8] = np.random.permutation(np.resize(levels, 8))
        for g in range(8):
            far = levels[np.abs(levels - a[p, g]) >= 10]
            a[p, g + 8] = far[np.random.randint(len(far))]
    return np.exp2(a.ravel()).repeat(32)


BF16 = ml_dtypes.bfloat16


def bf(x):
    return np.asarray(x, np.float32).astype(BF16)


def f64(x):
    return np.asarray(x).astype(np.float64)


M, K, N = 2048, 1024, 1024


def setup_inputs():
    s = mx_kscale(K)
    return {"guide": bf(np.random.standard_normal((M, K)) * s),
            "centre": bf(0.3 * np.random.standard_normal(K) * s),
            "width": bf((1.5 + 0.1 * np.random.standard_normal(K)) * s),
            "lum": bf(np.exp(0.5 * np.random.standard_normal(M))),
            "gain": bf(np.random.standard_normal((K, N)) / np.sqrt(K) / s[:, None]),
            "offset": bf(0.5 * np.random.standard_normal((K, N)) * np.exp(np.random.standard_normal((K, N)))
                         / np.sqrt(K) / s[:, None])}


def reference(guide, centre, width, lum, gain, offset):
    d = np.abs(f64(guide) - f64(centre))
    hat = np.maximum(f64(width) - d, 0.0)
    lit = hat * f64(lum)[:, None]
    hq = mxq(hat, 1, "e4m3")
    lq = mxq(lit, 1, "e4m3")
    gq = mxq(f64(gain), 0, "e4m3")
    oq = mxq(f64(offset), 0, "e5m2")
    return (lq @ gq) + (hq @ oq)

from contextlib import ExitStack

import concourse.mybir as mybir
from concourse.masks import make_identity

M, K, N = 2048, 1024, 1024
FLOPS = 2 * 2 * M * K * N

F32 = mybir.dt.float32
BF16 = mybir.dt.bfloat16
U32 = mybir.dt.uint32
U8 = mybir.dt.uint8
E4 = mybir.dt.float8_e4m3fn_x4
E5 = mybir.dt.float8_e5m2_x4
ALU = mybir.AluOpType
ACT = mybir.ActivationFunctionType

P = 128
CH = 512

ORDER = """
I:G,0,0,V tr:0,0,0 tr:0,0,1 A:0,0,0 A:0,0,1 A:0,0,2 A:0,0,3 QW:G,0,0 I:O,0,0,V tr:0,1,0 tr:0,1,1 A:0,1,0
A:0,1,1 A:0,1,2 A:0,1,3 B:0,0,0 B:0,0,1 B:0,0,2 B:0,0,3 QW:O,0,0 H:0,0,G C:0,0 B:0,1,0 B:0,1,1
B:0,1,2 B:0,1,3 QL:0,0 QH:0,0 I:G,0,1,V M:0,0,0,G,0 M:0,0,0,O,0 M:0,1,0,G,0 M:0,1,0,O,0 M:0,2,0,G,0 M:0,2,0,O,0 M:0,3,0,G,0
M:0,3,0,O,0 I:O,0,1,S H:0,1,G C:0,1 QW:G,0,1 I:G,1,0,S tr:1,0,0 tr:1,0,1 QW:O,0,1 A:1,0,0 A:1,0,1 A:1,0,2
A:1,0,3 QL:0,1 QH:0,1 I:O,1,0,S M:0,0,0,G,1 M:0,0,0,O,1 O:0,0,0,S M:0,1,0,G,1 M:0,1,0,O,1 O:0,1,0,S M:0,2,0,G,1 M:0,2,0,O,1
O:0,2,0,S M:0,3,0,G,1 M:0,3,0,O,1 O:0,3,0,S B:1,0,0 B:1,0,1 B:1,0,2 B:1,0,3 QW:G,1,0 H:1,0,G C:1,0 tr:1,1,0
tr:1,1,1 A:1,1,0 A:1,1,1 A:1,1,2 A:1,1,3 QW:O,1,0 I:O,1,1,V I:G,1,1,S M:0,0,1,G,0 M:0,0,1,O,0 M:0,1,1,G,0 M:0,1,1,O,0
M:0,2,1,G,0 M:0,2,1,O,0 M:0,3,1,G,0 M:0,3,1,O,0 QW:O,1,1 QL:1,0 QH:1,0 QW:G,1,1 B:1,1,0 B:1,1,1 B:1,1,2 B:1,1,3
tr:2,0,0 M:0,0,1,G,1 M:0,0,1,O,1 O:0,0,1,S M:0,1,1,G,1 M:0,1,1,O,1 O:0,1,1,S M:0,2,1,G,1 M:0,2,1,O,1 O:0,2,1,S M:0,3,1,G,1 M:0,3,1,O,1
O:0,3,1,S H:1,1,G C:1,1 tr:2,0,1 L:2 M:1,0,0,G,0 M:1,0,0,O,0 M:1,1,0,G,0 M:1,1,0,O,0 M:1,2,0,G,0 M:1,2,0,O,0 M:1,3,0,G,0 M:1,3,0,O,0
A:2,0,0 A:2,0,1 A:2,0,2 A:2,0,3 B:2,0,0 B:2,0,1 B:2,0,2 B:2,0,3 QL:1,1 QH:1,1 tr:2,1,0 tr:2,1,1
M:1,0,0,G,1 M:1,0,0,O,1 O:1,0,0,S M:1,1,0,G,1 M:1,1,0,O,1 O:1,1,0,S M:1,2,0,G,1 M:1,2,0,O,1 O:1,2,0,S M:1,3,0,G,1 M:1,3,0,O,1 O:1,3,0,S
A:2,1,0 A:2,1,1 A:2,1,2 A:2,1,3 M:1,0,1,G,0 M:1,0,1,O,0 M:1,1,1,G,0 M:1,1,1,O,0 M:1,2,1,G,0 M:1,2,1,O,0 M:1,3,1,G,0 M:1,3,1,O,0
H:2,0,G C:2,0 tr:3,0,0 M:1,0,1,G,1 M:1,0,1,O,1 O:1,0,1,S M:1,1,1,G,1 M:1,1,1,O,1 O:1,1,1,S M:1,2,1,G,1 M:1,2,1,O,1 O:1,2,1,S
M:1,3,1,G,1 M:1,3,1,O,1 O:1,3,1,S B:2,1,0 B:2,1,1 B:2,1,2 B:2,1,3 QL:2,0 QH:2,0 tr:3,0,1 L:3 A:3,0,0 A:3,0,1
A:3,0,2 A:3,0,3 H:2,1,G C:2,1 M:2,0,0,G,0 M:2,0,0,O,0 M:2,1,0,G,0 M:2,1,0,O,0 M:2,2,0,G,0 M:2,2,0,O,0 M:2,3,0,G,0 M:2,3,0,O,0
tr:3,1,0 tr:3,1,1 B:3,0,0 B:3,0,1 B:3,0,2 B:3,0,3 QL:2,1 QH:2,1 A:3,1,0 A:3,1,1 A:3,1,2 A:3,1,3
M:2,0,0,G,1 M:2,0,0,O,1 O:2,0,0,S M:2,1,0,G,1 M:2,1,0,O,1 O:2,1,0,S M:2,2,0,G,1 M:2,2,0,O,1 O:2,2,0,S M:2,3,0,G,1 M:2,3,0,O,1 O:2,3,0,S
M:2,0,1,G,0 M:2,0,1,O,0 M:2,1,1,G,0 M:2,1,1,O,0 M:2,2,1,G,0 M:2,2,1,O,0 M:2,3,1,G,0 M:2,3,1,O,0 H:3,0,G C:3,0 M:2,0,1,G,1 M:2,0,1,O,1
O:2,0,1,S M:2,1,1,G,1 M:2,1,1,O,1 O:2,1,1,S M:2,2,1,G,1 M:2,2,1,O,1 O:2,2,1,S M:2,3,1,G,1 M:2,3,1,O,1 O:2,3,1,S B:3,1,0 B:3,1,1
B:3,1,2 B:3,1,3 QL:3,0 QH:3,0 M:3,0,0,G,0 M:3,0,0,O,0 M:3,1,0,G,0 M:3,1,0,O,0 M:3,2,0,G,0 M:3,2,0,O,0 M:3,3,0,G,0 M:3,3,0,O,0
M:3,0,1,G,0 M:3,0,1,O,0 M:3,1,1,G,0 M:3,1,1,O,0 M:3,2,1,G,0 M:3,2,1,O,0 H:3,1,G C:3,1 QL:3,1 QH:3,1 M:3,0,0,G,1 M:3,0,0,O,1
O:3,0,0,S M:3,1,0,G,1 M:3,1,0,O,1 O:3,1,0,V M:3,2,0,G,1 M:3,2,0,O,1 O:3,2,0,S M:3,3,0,G,1 M:3,3,0,O,1 O:3,3,0,V M:3,0,1,G,1 M:3,0,1,O,1
M:3,1,1,G,1 M:3,1,1,O,1 M:3,2,1,G,1 M:3,2,1,O,1 O:3,0,1,S O:3,1,1,V O:3,2,1,S M:3,3,1,G,0 M:3,3,1,O,0 M:3,3,1,G,1 M:3,3,1,O,1 O:3,3,1,V

"""


def tile_hat_weighted_affine_s2_kernel(tc, guide, centre, width, lum, gain, offset, out):
    nc = tc.nc
    with ExitStack() as ctx:
        keep = ctx.enter_context(tc.tile_pool(name="keep", bufs=1))
        work = ctx.enter_context(tc.tile_pool(name="work", bufs=2))
        psum = ctx.enter_context(tc.psum_pool(name="psum", bufs=1))
        ctx.enter_context(tc.manual_schedule())

        tiles = {}

        lrow = keep.tile([P, P], BF16, align_bytes=64, name="lrow")
        nc.vector.memset(lrow[:], 0.0)
        identb = keep.tile([P, P], BF16, align_bytes=64, name="identb")
        identf = keep.tile([P, P], F32, align_bytes=64, name="identf")
        cc = keep.tile([P, 2, 4], BF16, align_bytes=64, name="cc")
        ww = keep.tile([P, 2, 4], BF16, align_bytes=64, name="ww")
        cneg = keep.tile([P, 8], F32, align_bytes=64, name="cneg")
        wid = keep.tile([P, 8], F32, align_bytes=64, name="wid")
        dummy = keep.tile([P, 1], F32, align_bytes=64, name="dummy")
        lt_sb = keep.tile([P, 16], BF16, align_bytes=64, name="lt_sb")
        nc.scalar.dma_start(out=cc[:], in_=centre.rearrange("(g p t) -> p g t", p=P, t=4))
        nc.scalar.dma_start(out=ww[:], in_=width.rearrange("(g p t) -> p g t", p=P, t=4))
        nc.scalar.dma_start(out=lrow[0:16, :], in_=lum.rearrange("(j n) -> j n", n=P))
        make_identity(nc, identf[:])
        make_identity(nc, identb[:])
        nc.gpsimd.memset(dummy[:], 0.0)

        for c in range(4):
            tiles["guide", c] = keep.tile([P, 4, K], BF16, align_bytes=64, name="guide" + str(c))
        for x in "GO":
            for h in range(2):
                for g in range(2):
                    tiles["raw", x, h, g] = keep.tile([P, 4, 512], BF16, align_bytes=64, name="raw" + x + str(h) + str(g))

        def load_guide(c, g0, g1):
            rows = guide[c * CH:(c + 1) * CH, g0 * 512:g1 * 512]
            nc.sync.dma_start(out=tiles["guide", c][:, :, g0 * 512:g1 * 512], in_=rows.rearrange("(q p) k -> p q k", p=P))

        def load_w(x, h, g):
            src = gain if x == "G" else offset
            rows = src[g * 512:(g + 1) * 512, h * 512:(h + 1) * 512]
            nc.sync.dma_start(out=tiles["raw", x, h, g][:], in_=rows.rearrange("(p j) n -> p j n", j=4))

        load_w("G", 0, 0)
        load_guide(0, 0, 1)
        load_w("O", 0, 0)
        load_guide(0, 1, 2)
        load_w("G", 0, 1)
        load_w("O", 0, 1)
        load_w("G", 1, 0)
        load_w("O", 1, 0)
        load_guide(1, 0, 2)
        load_w("G", 1, 1)
        load_w("O", 1, 1)
        load_guide(2, 0, 2)
        load_guide(3, 0, 2)

        nc.gpsimd.tensor_scalar(out=cneg[:], in0=cc[:].rearrange("p g t -> p (g t)"), scalar1=-1.0, scalar2=0.0, op0=ALU.mult, op1=ALU.add)
        nc.gpsimd.tensor_copy(out=wid[:], in_=ww[:].rearrange("p g t -> p (g t)"))
        nc.scalar.activation(out=dummy[:], in_=dummy[:], func=ACT.Abs)

        lt_ps = psum.tile([P, P], BF16, tag="tr", bufs=3, name="lt_ps")
        nc.tensor.transpose(lt_ps[:], lrow[:], identb[:])
        nc.vector.tensor_copy(out=lt_sb[:], in_=lt_ps[:, 0:16])

        lum_ps = psum.tile([P, 1024], BF16, tag="lum", bufs=1, name="lum_ps")

        def lum_chunk(c):
            for i in range(4):
                j = 4 * c + i
                w0 = (c % 2) * CH + i * P
                nc.tensor.transpose(lum_ps[:, w0:w0 + P], lt_sb[:, j:j + 1].to_broadcast([P, P]), identb[:])

        lum_chunk(0)
        lum_chunk(1)

        for tok in ORDER.split():
            kind = tok.split(":")[0]
            a = tok.split(":")[1].split(",")
            if kind == "L":
                lum_chunk(int(a[0]))
            if kind == "tr":
                c, g, u = int(a[0]), int(a[1]), int(a[2])
                words = tiles["guide", c][:].rearrange("p q k -> p (q k)").bitcast(F32)
                tp = psum.tile([P, CH], F32, tag="tr", bufs=3, name="tp")
                tiles["tr", c, g, u] = tp
                for q in range(4):
                    w0 = q * 512 + g * 256 + u
                    nc.tensor.transpose(tp[:, q * P:(q + 1) * P], words[:, w0:w0 + 255:2], identf[:])
            if kind == "A":
                c, g, t = int(a[0]), int(a[1]), int(a[2])
                if ("d", c, g) not in tiles:
                    tiles["d", c, g] = work.tile([P, 4, CH], F32, tag="d", bufs=4, align_bytes=64, name="d")
                src = tiles["tr", c, g, t // 2][:].bitcast(BF16).rearrange("p (m e) -> p m e", e=2)
                nc.scalar.activation(out=tiles["d", c, g][:, t, :], in_=src[:, :, t % 2], func=ACT.Abs, bias=cneg[:, 4 * g + t:4 * g + t + 1])
            if kind == "B":
                c, g, t = int(a[0]), int(a[1]), int(a[2])
                dt = tiles["d", c, g][:, t, :]
                nc.vector.tensor_scalar(out=dt, in0=dt, scalar1=wid[:, 4 * g + t:4 * g + t + 1], scalar2=0.0, op0=ALU.subtract, op1=ALU.min)
            if kind == "H":
                c, g, e = int(a[0]), int(a[1]), a[2]
                ht = work.tile([P, CH, 4], BF16, tag="hat", bufs=3, align_bytes=64, name="ht")
                tiles["hat", c, g] = ht
                src = tiles["d", c, g][:].rearrange("p t m -> p m t")
                if e == "S":
                    nc.scalar.activation(out=ht[:], in_=src, func=ACT.Copy, scale=-1.0)
                if e == "V":
                    nc.vector.tensor_scalar(out=ht[:], in0=src, scalar1=-1.0, scalar2=0.0, op0=ALU.mult, op1=ALU.add)
                if e == "G":
                    nc.gpsimd.tensor_scalar(out=ht[:], in0=src, scalar1=-1.0, scalar2=0.0, op0=ALU.mult, op1=ALU.add)
            if kind == "C":
                c, g = int(a[0]), int(a[1])
                ll = work.tile([P, CH, 4], BF16, tag="lit", bufs=3, align_bytes=64, name="ll")
                tiles["lit", c, g] = ll
                src = tiles["d", c, g][:].rearrange("p t m -> p m t")
                lv = lum_ps[:, (c % 2) * CH:(c % 2 + 1) * CH].unsqueeze(2).to_broadcast([P, CH, 4])
                nc.vector.scalar_tensor_tensor(out=ll[:], in0=src, scalar=-1.0, in1=lv, op0=ALU.mult, op1=ALU.mult)
            if kind == "QL" or kind == "QH":
                c, g = int(a[0]), int(a[1])
                nm = "lit" if kind == "QL" else "hat"
                x = "G" if kind == "QL" else "O"
                co = keep.tile([P, CH], U32, align_bytes=64, name="co" + nm + a[0] + a[1])
                sc = keep.tile([P, CH], U8, align_bytes=64, name="sc" + nm + a[0] + a[1])
                tiles["q", x, c, g] = (co, sc)
                nc.vector.quantize_mx(out=co[:].bitcast(E4), scales=sc[:], in_=tiles[nm, c, g][:].rearrange("p m t -> p (m t)"))
            if kind == "I":
                x, h, g, e = a[0], int(a[1]), int(a[2]), a[3]
                wg = work.tile([P, 512, 4], BF16, tag="wg", bufs=6, align_bytes=64, name="wg")
                tiles["wg", x, h, g] = wg
                src = tiles["raw", x, h, g][:].rearrange("p j n -> p n j")
                if e == "S":
                    nc.scalar.copy(out=wg[:], in_=src)
                if e == "V":
                    nc.vector.tensor_copy(out=wg[:], in_=src)
                if e == "G":
                    nc.gpsimd.tensor_scalar(out=wg[:], in0=src, scalar1=1.0, scalar2=0.0, op0=ALU.mult, op1=ALU.add)
            if kind == "QW":
                x, h, g = a[0], int(a[1]), int(a[2])
                co = keep.tile([P, 512], U32, align_bytes=64, name="wco" + a[0] + a[1] + a[2])
                sc = keep.tile([P, 512], U8, align_bytes=64, name="wsc" + a[0] + a[1] + a[2])
                tiles["wq", x, h, g] = (co, sc)
                nc.vector.quantize_mx(out=co[:].bitcast(E4 if x == "G" else E5), scales=sc[:], in_=tiles["wg", x, h, g][:].rearrange("p n j -> p (n j)"))
            if kind == "M":
                c, m, h, x, g = int(a[0]), int(a[1]), int(a[2]), a[3], int(a[4])
                key = ("acc", c, m, h)
                first = key not in tiles
                if first:
                    ng = len([k for k in tiles if k[0] == "acc"])
                    if 28 <= ng < 28 + 3:
                        acc = psum.tile([P, 512], F32, tag="tr", bufs=3, name="accx")
                    else:
                        acc = psum.tile([P, 512], F32, tag="acc", bufs=4, name="acc")
                    tiles[key] = acc
                    tiles["cnt", c, m, h] = 0
                cnt = tiles["cnt", c, m, h]
                tiles["cnt", c, m, h] = cnt + 1
                co, sc = tiles["q", x, c, g]
                wco, wsc = tiles["wq", x, h, g]
                nc.tensor.matmul_mx(
                    out=tiles[key][:],
                    lhsT=co[:, m * P:(m + 1) * P].bitcast(E4),
                    lhsT_scale=sc[:, m * P:(m + 1) * P],
                    rhs=wco[:].bitcast(E4 if x == "G" else E5),
                    rhs_scale=wsc[:],
                    start=(cnt == 0),
                    stop=(cnt == 3),
                )
            if kind == "O":
                c, m, h, e = int(a[0]), int(a[1]), int(a[2]), a[3]
                ot = work.tile([P, 512], F32, tag="ot", bufs=4, align_bytes=64, name="ot")
                if e == "S":
                    nc.scalar.copy(out=ot[:], in_=tiles["acc", c, m, h][:])
                else:
                    nc.vector.tensor_copy(out=ot[:], in_=tiles["acc", c, m, h][:])
                r0 = c * CH + m * P
                nc.sync.dma_start(out=out[r0:r0 + P, h * 512:(h + 1) * 512], in_=ot[:])
